import numpy as np
import ml_dtypes


def mxq(x, axis, fmt="e4m3"):
    dtype, down = {"e4m3": (ml_dtypes.float8_e4m3fn, 7), "e5m2": (ml_dtypes.float8_e5m2, 14)}[fmt]
    v = np.moveaxis(np.asarray(x, np.float32).astype(ml_dtypes.bfloat16).astype(np.float64), axis, -1)
    blocks = v.reshape(v.shape[:-1] + (-1, 32))
    amax = np.abs(blocks).max(-1, keepdims=True)
    byte = np.maximum(np.where(amax > 0, np.frexp(amax)[1] - 1 + 127, 0) - down, 1)
    scale = np.exp2(byte - 127.0)
    codes = (blocks / scale).astype(np.float32).astype(dtype).astype(np.float64)
    return np.moveaxis((codes * scale).reshape(v.shape), -1, axis)


WIDE = False


def mx_kscale(k):
    if not WIDE:
        return np.ones(k)
    levels = np.array([10, -10, 5, -5, 0])
    if k % 512:
        return np.exp2(np.random.permutation(np.resize(levels, k // 32))).repeat(32)
    a = np.empty((k // 512, 16))
    for p in range(k // 512):
        a[p, :8] = np.random.permutation(np.resize(levels, 8))
        for g in range(8):
            far = levels[np.abs(levels - a[p, g]) >= 10]
            a[p, g + 8] = far[np.random.randint(len(far))]
    return np.exp2(a.ravel()).repeat(32)


def f64(x):
    return np.asarray(x).astype(np.float64)


def striped(idx):
    return np.tile(idx.reshape(-1, 16).T, (8, 1)).astype(np.uint16)


def unstriped(offs):
    return offs[:16].T.reshape(-1).astype(np.int64)


def pack_weight(w):
    k, n = w.shape
    w = f64(np.asarray(w, np.float32).astype(ml_dtypes.bfloat16)).reshape(k // 32, 32, n)
    amax = np.abs(w).max(1)
    byte = np.clip(np.where(amax > 0, np.frexp(amax)[1] - 1 + 127 - 7, 1), 1, 254)
    scaled = (w * np.exp2(127.0 - byte)[:, None, :]).reshape(k, n).astype(np.float32)
    words = np.ascontiguousarray(scaled.reshape(k // 512, 128, 4, n).transpose(0, 1, 3, 2)).astype(ml_dtypes.float8_e4m3fn).view(np.uint8)
    return words, np.ascontiguousarray(byte.astype(np.uint8).reshape(k // 512, 16, n))


def unpack_weight(words, scales):
    g, p, n, _ = words.shape
    vals = np.ascontiguousarray(words).view(ml_dtypes.float8_e4m3fn).astype(np.float64) * np.repeat(np.exp2(scales.astype(np.float64) - 127.0), 8, axis=1)[..., None]
    return vals.transpose(0, 1, 3, 2).reshape(g * 512, n)


K, T, S, N, H, U = 1024, 1024, 512, 128, 512, 1024


def setup_inputs():
    n = np.random.standard_normal
    s = mx_kscale(K)[:, None]
    u = mx_kscale(H)
    packed_xT = pack_weight(n((K, T)) * s)
    return {
        "x_words": packed_xT[0],
        "x_scales": packed_xT[1],
        "w1": (n((K, H)) / np.sqrt(K) / s).astype(np.float32),
        "w2": (n((K, H)) / np.sqrt(K) / s).astype(np.float32),
        "arr": (n((H, U))).astype(np.float32),
        "unit": (np.random.uniform(0.6, 1.4, (H, 1)) * u[:, None]).astype(np.float32),
        "w3": (n((H, N)) / np.sqrt(H) / u[:, None]).astype(np.float32),
        "offs": striped(np.random.permutation(T)[:S]),
        "bk": striped(np.random.permutation(np.concatenate([np.arange(S), np.random.randint(0, S, U - S)]))),
        "rw_": striped(np.random.permutation(np.concatenate([np.arange(S), np.random.randint(0, S, U - S)]))),
    }


def reference(x_words, x_scales, w1, w2, arr, unit, w3, offs, bk, rw_):
    xq = unpack_weight(x_words, x_scales)[:, unstriped(offs)]
    y = mxq(f64(w1), 0, "e4m3").T @ xq
    yk = y[:, unstriped(bk)]
    yr = y[:, unstriped(rw_)]
    busy = np.maximum(yk, yr)
    z1 = mxq(f64(w2), 0, "e4m3").T @ xq
    zk = z1[:, unstriped(bk)]
    rdy = np.maximum(busy, zk)
    hid = f64(unit) * (rdy - f64(arr))
    return mxq(f64(w3), 0, "e4m3").T @ mxq(hid, 0, "e4m3")

@@ -1,0 +1,235 @@
+from contextlib import ExitStack
+
+import concourse.mybir as mybir
+
+K, T, S, N, H, U = 1024, 1024, 512, 128, 512, 1024
+FLOPS = 2 * (2 * K * H * S + H * N * U)
+
+F32 = mybir.dt.float32
+BF16 = mybir.dt.bfloat16
+I32 = mybir.dt.int32
+U32 = mybir.dt.uint32
+U16 = mybir.dt.uint16
+U8 = mybir.dt.uint8
+FP8X4 = mybir.dt.float8_e4m3fn_x4
+ALU = mybir.AluOpType
+ACT = mybir.ActivationFunctionType
+
+P = 128
+PACK = 4
+K_PASS = P * PACK
+PASSES = K // K_PASS
+CHUNKS = (384, 256, 256, 128)
+RING = 3
+ROW_RING = 2
+
+
+def tile_picked_ydelayq_wait_p_kernel(tc, x_words, x_scales, w1, w2, arr, unit, w3, offs, bk, rw_, out):
+    nc = tc.nc
+    with ExitStack() as ctx:
+        keep = ctx.enter_context(tc.tile_pool(name="keep", bufs=1))
+        ring = ctx.enter_context(tc.tile_pool(name="ring", bufs=RING))
+        psum = ctx.enter_context(tc.psum_pool(name="psum", bufs=1))
+
+        offs_sb = keep.tile([P, S // 16], U16, name="offs_sb")
+        bk_sb = keep.tile([P, U // 16], U16, name="bk_sb")
+        rw_sb = keep.tile([P, U // 16], U16, name="rw_sb")
+        xs_all = keep.tile([P, T], U8, name="xs_all", align_bytes=64)
+        unit_sb = keep.tile([P, PACK], F32, name="unit_sb")
+        xw_all = [keep.tile([P, T], U32, name=f"xw_all{g}", align_bytes=64) for g in range(PASSES)]
+
+        nc.gpsimd.memset(xs_all[:].bitcast(I32), 0)
+        nc.sync.dma_start(offs_sb[:], offs)
+
+        def load_x(g):
+            nc.sync.dma_start(xw_all[g][:].bitcast(I32), x_words[g].rearrange("p n t -> p (n t)").bitcast(I32))
+
+        def load_w(w, name, g, c0, c1):
+            raw = keep.tile([P, PACK, c1 - c0], F32, name=f"{name}_raw{g}_{c0}", align_bytes=64)
+            rows = w[g * K_PASS : (g + 1) * K_PASS, c0:c1]
+            nc.sync.dma_start(raw[:], rows.rearrange("(p j) c -> p j c", j=PACK))
+            return raw
+
+        load_x(0)
+        for q in range(4):
+            nc.sync.dma_start(
+                xs_all[32 * q : 32 * q + 4 * PASSES, :].bitcast(I32),
+                x_scales[:, 4 * q : 4 * q + 4, :].bitcast(I32),
+            )
+        nc.sync.dma_start(unit_sb[:], unit.rearrange("(p t) o -> p (t o)", t=PACK))
+        w1_raw0 = [load_w(w1, "w1", 0, c0, c0 + H // 2) for c0 in (0, H // 2)]
+        load_x(1)
+        nc.sync.dma_start(rw_sb[:], rw_)
+        w1_raw1 = [load_w(w1, "w1", 1, c0, c0 + H // 2) for c0 in (0, H // 2)]
+        nc.sync.dma_start(bk_sb[:], bk)
+        w2_raw0 = load_w(w2, "w2", 0, 0, H)
+        w2_raw1 = [load_w(w2, "w2", 1, c0, c0 + H // 2) for c0 in (0, H // 2)]
+        w3_raw = load_w(w3, "w3", 0, 0, N)
+        arr_sb = []
+        r0 = 0
+        for c, n in enumerate(CHUNKS):
+            a = keep.tile([P, PACK, n], F32, name=f"arr{c}", align_bytes=64)
+            nc.sync.dma_start(a[:], arr[:, r0 : r0 + n].rearrange("(p t) r -> p t r", t=PACK))
+            arr_sb.append(a)
+            r0 = r0 + n
+
+        size = keep.tile([P, PACK], F32, name="size")
+        neg_size = keep.tile([P, PACK], F32, name="neg_size")
+        step = keep.tile([P, PACK], F32, name="step")
+        sign = keep.tile([P, PACK], F32, name="sign")
+        nc.scalar.activation(size[:], unit_sb[:], ACT.Abs)
+        nc.scalar.activation(neg_size[:], size[:], ACT.Copy, scale=-1.0)
+        nc.vector.tensor_scalar(step[:], unit_sb[:], 0.0, 2.0, ALU.is_ge, ALU.mult)
+        nc.vector.tensor_scalar(sign[:], step[:], -1.0, None, ALU.add)
+
+        xw = [keep.tile([P, S], U32, name=f"xw{g}", align_bytes=64) for g in range(PASSES)]
+        xs = keep.tile([P, S], U8, name="xs", align_bytes=64)
+
+        def gather_x(g):
+            nc.vector.tensor_copy(xw[g][:], xw_all[g][:].indirect(offs_sb[:]))
+
+        def new_weight(name):
+            grouped = keep.tile([P, PACK, P, PACK], BF16, name=f"{name}_bf", align_bytes=64)
+            codes = keep.tile([P, H], U32, name=f"{name}_codes", align_bytes=64)
+            scales = keep.tile([P, H], U8, name=f"{name}_scales", align_bytes=64)
+            return grouped, codes, scales
+
+        def cast(copy, weight, raw, raw_m0, m0, m1):
+            src = raw[:].rearrange("p j (m t) -> p m j t", t=PACK)[:, m0 - raw_m0 : m1 - raw_m0]
+            dst = weight[0][:].rearrange("p t m j -> p m j t")[:, m0:m1]
+            copy(dst, src)
+
+        def quantize(weight, t0, t1):
+            grouped, codes, scales = weight
+            nc.vector.quantize_mx(
+                codes[:, t0 * P : t1 * P].bitcast(FP8X4),
+                scales[:, t0 * P : t1 * P],
+                grouped[:, t0:t1].rearrange("p t m j -> p (t m j)"),
+            )
+
+        def product(bank, weight, g, t):
+            nc.tensor.matmul_mx(
+                bank[:],
+                lhsT=weight[1][:, t * P : (t + 1) * P].bitcast(FP8X4),
+                lhsT_scale=weight[2][:, t * P : (t + 1) * P],
+                rhs=xw[g][:].bitcast(FP8X4),
+                rhs_scale=xs[4 * g : P, :],
+                start=(g == 0),
+                stop=(g == PASSES - 1),
+            )
+
+        vcopy, scopy = nc.vector.tensor_copy, nc.scalar.copy
+        ybank = [psum.tile([P, S], F32, name=f"ybank{t}", tag=f"bank{t}") for t in range(PACK)]
+        zbank = [psum.tile([P, S], F32, name=f"zbank{t}", tag=f"bank{PACK + t}") for t in range(PACK)]
+        y_sb = [keep.tile([P, S], F32, name=f"y_sb{t}", align_bytes=64) for t in range(PACK)]
+        m_sb = [keep.tile([P, S], F32, name=f"m_sb{t}", align_bytes=64) for t in range(PACK)]
+
+        gather_x(0)
+        nc.vector.tensor_copy(xs[:], xs_all[:].indirect(offs_sb[:]))
+        w1q0 = new_weight("w1q0")
+        cast(scopy, w1q0, w1_raw0[0], 0, 0, 64)
+        cast(vcopy, w1q0, w1_raw0[1], 64, 64, 128)
+        quantize(w1q0, 0, PACK)
+        for t in range(PACK):
+            product(ybank[t], w1q0, 0, t)
+        gather_x(1)
+        w1q1 = new_weight("w1q1")
+        cast(scopy, w1q1, w1_raw1[0], 0, 0, 64)
+        cast(scopy, w1q1, w1_raw1[1], 64, 64, 86)
+        cast(vcopy, w1q1, w1_raw1[1], 64, 86, 128)
+        for t in range(PACK):
+            quantize(w1q1, t, t + 1)
+            product(ybank[t], w1q1, 1, t)
+            if t not in (1, 3,):
+                nc.scalar.activation(y_sb[t][:], ybank[t][:], ACT.Copy, scale=size[:, t : t + 1])
+            else:
+                nc.vector.tensor_scalar(y_sb[t][:], ybank[t][:], size[:, t : t + 1], None, ALU.mult)
+
+        w2q0 = new_weight("w2q0")
+        cast(vcopy, w2q0, w2_raw0, 0, 0, 128)
+        quantize(w2q0, 0, PACK)
+        for t in range(PACK):
+            product(zbank[t], w2q0, 0, t)
+        w2q1 = new_weight("w2q1")
+        cast(vcopy, w2q1, w2_raw1[0], 0, 0, 64)
+        cast(vcopy, w2q1, w2_raw1[1], 64, 64, 128)
+        for t in range(PACK):
+            quantize(w2q1, t, t + 1)
+            product(zbank[t], w2q1, 1, t)
+
+        w3_bf = keep.tile([P, N, PACK], BF16, name="w3_bf", align_bytes=64)
+        w3_codes = keep.tile([P, N], U32, name="w3_codes", align_bytes=64)
+        w3_scales = keep.tile([P, N], U8, name="w3_scales", align_bytes=64)
+        nc.vector.tensor_tensor(
+            w3_bf[:].rearrange("p (c i) j -> p c j i", i=2),
+            w3_raw[:].rearrange("p j (c i) -> p c j i", i=2),
+            sign[:].rearrange("p (c j i) -> p c j i", c=1, i=1).to_broadcast([P, N // 2, PACK, 2]),
+            ALU.mult,
+        )
+        for t in range(PACK):
+            nc.vector.scalar_tensor_tensor(
+                m_sb[t][:], zbank[t][:], size[:, t : t + 1], y_sb[t][:], ALU.mult, ALU.max
+            )
+        nc.vector.quantize_mx(w3_codes[:].bitcast(FP8X4), w3_scales[:], w3_bf[:].rearrange("p n j -> p (n j)"))
+
+
+        starts = [sum(CHUNKS[:c]) for c in range(len(CHUNKS))]
+        by_row = {}
+
+        def look_up(on_vector, dst, window, offsets):
+            if on_vector:
+                nc.vector.tensor_copy(dst, window.indirect(offsets))
+            else:
+                nc.scalar.activation(dst, window.indirect(offsets), ACT.Copy)
+
+        def fetch_rows(c):
+            n = CHUNKS[c]
+            cols = slice(starts[c] // 16, (starts[c] + n) // 16)
+            by_row[c] = ring.tile([P, PACK, n], F32, name="by_row", align_bytes=64, bufs=ROW_RING)
+            for t in range(PACK):
+                look_up(c in (3,), by_row[c][:, t, :], y_sb[t][:], rw_sb[:, cols])
+
+        fetch_rows(0)
+        fetch_rows(1)
+        for c, n in enumerate(CHUNKS):
+            r0 = starts[c]
+            cols = slice(r0 // 16, (r0 + n) // 16)
+            by_bank = ring.tile([P, PACK, n], F32, name="by_bank", align_bytes=64)
+            ready = ring.tile([P, PACK, n], F32, name="ready", align_bytes=64)
+            hid = ring.tile([P, PACK, n], BF16, name="hid", align_bytes=64)
+            hid_grouped = ring.tile([P, n, PACK], BF16, name="hid_grouped", align_bytes=64)
+            hid_codes = ring.tile([P, n], U32, name="hid_codes", align_bytes=64)
+            hid_scales = ring.tile([P, n], U8, name="hid_scales", align_bytes=64)
+            result = ring.tile([P, n], F32, name="result", align_bytes=64)
+            for t in range(PACK):
+                look_up(c in (), by_bank[:, t, :], m_sb[t][:], bk_sb[:, cols])
+            for t in range(PACK + 1):
+                if t < PACK:
+                    nc.vector.tensor_tensor(ready[:, t, :], by_row[c][:, t, :], by_bank[:, t, :], ALU.max)
+                if t > 0:
+                    nc.vector.scalar_tensor_tensor(
+                        hid[:, t - 1, :], arr_sb[c][:, t - 1, :], neg_size[:, t - 1 : t], ready[:, t - 1, :], ALU.mult, ALU.add
+                    )
+            nc.vector.tensor_copy(
+                hid_grouped[:].rearrange("p (c i) t -> p c t i", i=4),
+                hid[:].rearrange("p t (c i) -> p c t i", i=4),
+            )
+            nc.vector.quantize_mx(
+                hid_codes[:].bitcast(FP8X4), hid_scales[:], hid_grouped[:].rearrange("p r t -> p (r t)")
+            )
+            if c + 2 < len(CHUNKS):
+                fetch_rows(c + 2)
+            obank = psum.tile([P, S], F32, name=f"obank{c}", tag=f"bank{c % PACK}")
+            for n0 in range(0, n, 256):
+                n1 = min(n, n0 + 256)
+                nc.tensor.matmul_mx(
+                    obank[:, n0:n1],
+                    lhsT=w3_codes[:].bitcast(FP8X4),
+                    lhsT_scale=w3_scales[:],
+                    rhs=hid_codes[:, n0:n1].bitcast(FP8X4),
+                    rhs_scale=hid_scales[:, n0:n1],
+                    start=True,
+                    stop=True,
+                )
+            nc.scalar.copy(result[:], obank[:, 0:n])
+            nc.sync.dma_start(out[:, r0 : r0 + n], result[:])

@@ -19,7 +19,7 @@ P = 128
 PACK = 4
 K_PASS = P * PACK
 PASSES = K // K_PASS
-CHUNKS = (384, 256, 256, 128)
+CHUNKS = (256, 384, 256, 128)
 RING = 3
 ROW_RING = 2
 
@@ -35,76 +35,76 @@ def tile_picked_ydelayq_wait_p_kernel(tc, x_words, x_scales, w1, w2, arr, unit, 
         bk_sb = keep.tile([P, U // 16], U16, name="bk_sb")
         rw_sb = keep.tile([P, U // 16], U16, name="rw_sb")
         xs_all = keep.tile([P, T], U8, name="xs_all", align_bytes=64)
-        unit_sb = keep.tile([P, PACK], F32, name="unit_sb")
+        unit_sb = keep.tile([P, 2 * PACK - 1], F32, name="unit_sb")
         xw_all = [keep.tile([P, T], U32, name=f"xw_all{g}", align_bytes=64) for g in range(PASSES)]
-
-        nc.gpsimd.memset(xs_all[:].bitcast(I32), 0)
-        nc.sync.dma_start(offs_sb[:], offs)
+        w1_raw = [keep.tile([P, PACK, H], F32, name=f"w1_raw{g}", align_bytes=64) for g in range(PASSES)]
+        w2_raw = [keep.tile([P, PACK, H], F32, name=f"w2_raw{g}", align_bytes=64) for g in range(PASSES)]
+        w3_raw = keep.tile([P, PACK, N], F32, name="w3_raw", align_bytes=64)
+        arr_sb = keep.tile([P, PACK, U], F32, name="arr_sb", align_bytes=64)
 
         def load_x(g):
             nc.sync.dma_start(xw_all[g][:].bitcast(I32), x_words[g].rearrange("p n t -> p (n t)").bitcast(I32))
 
-        def load_w(w, name, g, c0, c1):
-            raw = keep.tile([P, PACK, c1 - c0], F32, name=f"{name}_raw{g}_{c0}", align_bytes=64)
-            rows = w[g * K_PASS : (g + 1) * K_PASS, c0:c1]
-            nc.sync.dma_start(raw[:], rows.rearrange("(p j) c -> p j c", j=PACK))
-            return raw
+        def load_w(raw, w, g):
+            nc.sync.dma_start(raw[g][:], w[g * K_PASS : (g + 1) * K_PASS, :].rearrange("(p j) c -> p j c", j=PACK))
 
+        nc.gpsimd.memset(xs_all[:].bitcast(I32), 0)
+        nc.sync.dma_start(offs_sb[:], offs)
         load_x(0)
         for q in range(4):
             nc.sync.dma_start(
                 xs_all[32 * q : 32 * q + 4 * PASSES, :].bitcast(I32),
                 x_scales[:, 4 * q : 4 * q + 4, :].bitcast(I32),
             )
-        nc.sync.dma_start(unit_sb[:], unit.rearrange("(p t) o -> p (t o)", t=PACK))
-        w1_raw0 = [load_w(w1, "w1", 0, c0, c0 + H // 2) for c0 in (0, H // 2)]
+        load_w(w1_raw, w1, 0)
         load_x(1)
+        unit_rows = unit.rearrange("(a s) o -> a (s o)", s=2 * PACK)
+        for e in range(2):
+            nc.sync.dma_start(unit_sb[e:P:2, :], unit_rows[:, e : e + 2 * PACK - 1])
+        load_w(w1_raw, w1, 1)
         nc.sync.dma_start(rw_sb[:], rw_)
-        w1_raw1 = [load_w(w1, "w1", 1, c0, c0 + H // 2) for c0 in (0, H // 2)]
+        load_w(w2_raw, w2, 0)
+        load_w(w2_raw, w2, 1)
         nc.sync.dma_start(bk_sb[:], bk)
-        w2_raw0 = load_w(w2, "w2", 0, 0, H)
-        w2_raw1 = [load_w(w2, "w2", 1, c0, c0 + H // 2) for c0 in (0, H // 2)]
-        w3_raw = load_w(w3, "w3", 0, 0, N)
-        arr_sb = []
-        r0 = 0
-        for c, n in enumerate(CHUNKS):
-            a = keep.tile([P, PACK, n], F32, name=f"arr{c}", align_bytes=64)
-            nc.sync.dma_start(a[:], arr[:, r0 : r0 + n].rearrange("(p t) r -> p t r", t=PACK))
-            arr_sb.append(a)
-            r0 = r0 + n
+        for e in range(2):
+            nc.sync.dma_start(w3_raw[e:P:2], w3.rearrange("(a t e) n -> e a t n", t=PACK, e=2)[e])
+        for t in range(PACK):
+            nc.sync.dma_start(arr_sb[:, t, :], arr.rearrange("(a t e) r -> t a e r", t=PACK, e=2)[t])
 
+        unit_t = unit_sb[:, 0 : 2 * PACK - 1 : 2]
         size = keep.tile([P, PACK], F32, name="size")
-        neg_size = keep.tile([P, PACK], F32, name="neg_size")
         step = keep.tile([P, PACK], F32, name="step")
         sign = keep.tile([P, PACK], F32, name="sign")
-        nc.scalar.activation(size[:], unit_sb[:], ACT.Abs)
-        nc.scalar.activation(neg_size[:], size[:], ACT.Copy, scale=-1.0)
-        nc.vector.tensor_scalar(step[:], unit_sb[:], 0.0, 2.0, ALU.is_ge, ALU.mult)
-        nc.vector.tensor_scalar(sign[:], step[:], -1.0, None, ALU.add)
+        nc.scalar.activation(size[:], unit_t, ACT.Abs)
+        nc.gpsimd.tensor_scalar(step[:], unit_t, 0.0, 2.0, ALU.is_ge, ALU.mult)
+        nc.gpsimd.tensor_scalar(sign[:], step[:], 1.0, -1.0, ALU.mult, ALU.add)
 
-        xw = [keep.tile([P, S], U32, name=f"xw{g}", align_bytes=64) for g in range(PASSES)]
+        xw = {}
         xs = keep.tile([P, S], U8, name="xs", align_bytes=64)
 
-        def gather_x(g):
+        def gather_x(g, tag):
+            xw[g] = keep.tile([P, S], U32, name=f"xw{g}", tag=tag, align_bytes=64)
             nc.vector.tensor_copy(xw[g][:], xw_all[g][:].indirect(offs_sb[:]))
 
         def new_weight(name):
-            grouped = keep.tile([P, PACK, P, PACK], BF16, name=f"{name}_bf", align_bytes=64)
+            grouped = [keep.tile([P, P, PACK], BF16, name=f"{name}_bf{t}", tag=f"{name}_bf{t}", align_bytes=64) for t in range(PACK)]
             codes = keep.tile([P, H], U32, name=f"{name}_codes", align_bytes=64)
             scales = keep.tile([P, H], U8, name=f"{name}_scales", align_bytes=64)
             return grouped, codes, scales
 
-        def cast(copy, weight, raw, raw_m0, m0, m1):
-            src = raw[:].rearrange("p j (m t) -> p m j t", t=PACK)[:, m0 - raw_m0 : m1 - raw_m0]
-            dst = weight[0][:].rearrange("p t m j -> p m j t")[:, m0:m1]
-            copy(dst, src)
+        def cast(on_vector, weight, raw, t):
+            copy = nc.vector.tensor_copy if on_vector else nc.scalar.copy
+            copy(
+                weight[0][t][:].rearrange("p (a e) j -> p a j e", e=2),
+                raw[:].rearrange("p j (a t e) -> p t a j e", t=PACK, e=2)[:, t],
+            )
 
-        def quantize(weight, t0, t1):
+        def quantize(weight, t):
             grouped, codes, scales = weight
             nc.vector.quantize_mx(
-                codes[:, t0 * P : t1 * P].bitcast(FP8X4),
-                scales[:, t0 * P : t1 * P],
-                grouped[:, t0:t1].rearrange("p t m j -> p (t m j)"),
+                codes[:, t * P : (t + 1) * P].bitcast(FP8X4),
+                scales[:, t * P : (t + 1) * P],
+                grouped[t][:].rearrange("p m j -> p (m j)"),
             )
 
         def product(bank, weight, g, t):
@@ -118,44 +118,46 @@ def tile_picked_ydelayq_wait_p_kernel(tc, x_words, x_scales, w1, w2, arr, unit, 
                 stop=(g == PASSES - 1),
             )
 
-        vcopy, scopy = nc.vector.tensor_copy, nc.scalar.copy
+        def weight_pass(banks, name, raw, g, on_vector):
+            weight = new_weight(name)
+            for t in range(PACK + 1):
+                if t < PACK:
+                    cast(t in on_vector, weight, raw[g], t)
+                if t > 0:
+                    quantize(weight, t - 1)
+                    product(banks[t - 1], weight, g, t - 1)
+
+        def wide_pass(banks, name, raw, g):
+            grouped = keep.tile([P, PACK, P, PACK], BF16, name=f"{name}_bf", align_bytes=64)
+            codes = keep.tile([P, H], U32, name=f"{name}_codes", align_bytes=64)
+            scales = keep.tile([P, H], U8, name=f"{name}_scales", align_bytes=64)
+            nc.vector.tensor_copy(
+                grouped[:].rearrange("p t (a e) j -> p a t j e", e=2),
+                raw[g][:].rearrange("p j (a t e) -> p a t j e", t=PACK, e=2),
+            )
+            nc.vector.quantize_mx(codes[:].bitcast(FP8X4), scales[:], grouped[:].rearrange("p t m j -> p (t m j)"))
+            for t in range(PACK):
+                product(banks[t], (grouped, codes, scales), g, t)
+
         ybank = [psum.tile([P, S], F32, name=f"ybank{t}", tag=f"bank{t}") for t in range(PACK)]
         zbank = [psum.tile([P, S], F32, name=f"zbank{t}", tag=f"bank{PACK + t}") for t in range(PACK)]
         y_sb = [keep.tile([P, S], F32, name=f"y_sb{t}", align_bytes=64) for t in range(PACK)]
         m_sb = [keep.tile([P, S], F32, name=f"m_sb{t}", align_bytes=64) for t in range(PACK)]
 
-        gather_x(0)
+        gather_x(0, "xw0")
         nc.vector.tensor_copy(xs[:], xs_all[:].indirect(offs_sb[:]))
-        w1q0 = new_weight("w1q0")
-        cast(scopy, w1q0, w1_raw0[0], 0, 0, 64)
-        cast(vcopy, w1q0, w1_raw0[1], 64, 64, 128)
-        quantize(w1q0, 0, PACK)
+        weight_pass(ybank, "w1q0", w1_raw, 0, (1, 3,))
+        gather_x(1, "w1q0_bf3")
+        weight_pass(ybank, "w1q1", w1_raw, 1, (0, 2,))
         for t in range(PACK):
-            product(ybank[t], w1q0, 0, t)
-        gather_x(1)
-        w1q1 = new_weight("w1q1")
-        cast(scopy, w1q1, w1_raw1[0], 0, 0, 64)
-        cast(scopy, w1q1, w1_raw1[1], 64, 64, 86)
-        cast(vcopy, w1q1, w1_raw1[1], 64, 86, 128)
-        for t in range(PACK):
-            quantize(w1q1, t, t + 1)
-            product(ybank[t], w1q1, 1, t)
-            if t not in (1, 3,):
-                nc.scalar.activation(y_sb[t][:], ybank[t][:], ACT.Copy, scale=size[:, t : t + 1])
-            else:
+            if t in (1,):
                 nc.vector.tensor_scalar(y_sb[t][:], ybank[t][:], size[:, t : t + 1], None, ALU.mult)
-
-        w2q0 = new_weight("w2q0")
-        cast(vcopy, w2q0, w2_raw0, 0, 0, 128)
-        quantize(w2q0, 0, PACK)
+            else:
+                nc.scalar.activation(y_sb[t][:], ybank[t][:], ACT.Copy, scale=size[:, t : t + 1])
+        wide_pass(zbank, "w2q0", w2_raw, 0)
+        weight_pass(zbank, "w2q1", w2_raw, 1, range(PACK))
         for t in range(PACK):
-            product(zbank[t], w2q0, 0, t)
-        w2q1 = new_weight("w2q1")
-        cast(vcopy, w2q1, w2_raw1[0], 0, 0, 64)
-        cast(vcopy, w2q1, w2_raw1[1], 64, 64, 128)
-        for t in range(PACK):
-            quantize(w2q1, t, t + 1)
-            product(zbank[t], w2q1, 1, t)
+            nc.vector.scalar_tensor_tensor(m_sb[t][:], zbank[t][:], size[:, t : t + 1], y_sb[t][:], ALU.mult, ALU.max)
 
         w3_bf = keep.tile([P, N, PACK], BF16, name="w3_bf", align_bytes=64)
         w3_codes = keep.tile([P, N], U32, name="w3_codes", align_bytes=64)
@@ -166,15 +168,10 @@ def tile_picked_ydelayq_wait_p_kernel(tc, x_words, x_scales, w1, w2, arr, unit, 
             sign[:].rearrange("p (c j i) -> p c j i", c=1, i=1).to_broadcast([P, N // 2, PACK, 2]),
             ALU.mult,
         )
-        for t in range(PACK):
-            nc.vector.scalar_tensor_tensor(
-                m_sb[t][:], zbank[t][:], size[:, t : t + 1], y_sb[t][:], ALU.mult, ALU.max
-            )
         nc.vector.quantize_mx(w3_codes[:].bitcast(FP8X4), w3_scales[:], w3_bf[:].rearrange("p n j -> p (n j)"))
 
-
         starts = [sum(CHUNKS[:c]) for c in range(len(CHUNKS))]
-        by_row = {}
+        by_row, hid_grouped = {}, {}
 
         def look_up(on_vector, dst, window, offsets):
             if on_vector:
@@ -187,38 +184,16 @@ def tile_picked_ydelayq_wait_p_kernel(tc, x_words, x_scales, w1, w2, arr, unit, 
             cols = slice(starts[c] // 16, (starts[c] + n) // 16)
             by_row[c] = ring.tile([P, PACK, n], F32, name="by_row", align_bytes=64, bufs=ROW_RING)
             for t in range(PACK):
-                look_up(c in (3,), by_row[c][:, t, :], y_sb[t][:], rw_sb[:, cols])
+                look_up((c, t) in (), by_row[c][:, t, :], y_sb[t][:], rw_sb[:, cols])
 
-        fetch_rows(0)
-        fetch_rows(1)
-        for c, n in enumerate(CHUNKS):
-            r0 = starts[c]
-            cols = slice(r0 // 16, (r0 + n) // 16)
-            by_bank = ring.tile([P, PACK, n], F32, name="by_bank", align_bytes=64)
-            ready = ring.tile([P, PACK, n], F32, name="ready", align_bytes=64)
-            hid = ring.tile([P, PACK, n], BF16, name="hid", align_bytes=64)
-            hid_grouped = ring.tile([P, n, PACK], BF16, name="hid_grouped", align_bytes=64)
+        def finish(c):
+            n, r0 = CHUNKS[c], starts[c]
             hid_codes = ring.tile([P, n], U32, name="hid_codes", align_bytes=64)
             hid_scales = ring.tile([P, n], U8, name="hid_scales", align_bytes=64)
             result = ring.tile([P, n], F32, name="result", align_bytes=64)
-            for t in range(PACK):
-                look_up(c in (), by_bank[:, t, :], m_sb[t][:], bk_sb[:, cols])
-            for t in range(PACK + 1):
-                if t < PACK:
-                    nc.vector.tensor_tensor(ready[:, t, :], by_row[c][:, t, :], by_bank[:, t, :], ALU.max)
-                if t > 0:
-                    nc.vector.scalar_tensor_tensor(
-                        hid[:, t - 1, :], arr_sb[c][:, t - 1, :], neg_size[:, t - 1 : t], ready[:, t - 1, :], ALU.mult, ALU.add
-                    )
-            nc.vector.tensor_copy(
-                hid_grouped[:].rearrange("p (c i) t -> p c t i", i=4),
-                hid[:].rearrange("p t (c i) -> p c t i", i=4),
-            )
             nc.vector.quantize_mx(
-                hid_codes[:].bitcast(FP8X4), hid_scales[:], hid_grouped[:].rearrange("p r t -> p (r t)")
+                hid_codes[:].bitcast(FP8X4), hid_scales[:], hid_grouped[c][:].rearrange("p r t -> p (r t)")
             )
-            if c + 2 < len(CHUNKS):
-                fetch_rows(c + 2)
             obank = psum.tile([P, S], F32, name=f"obank{c}", tag=f"bank{c % PACK}")
             for n0 in range(0, n, 256):
                 n1 = min(n, n0 + 256)
@@ -233,3 +208,30 @@ def tile_picked_ydelayq_wait_p_kernel(tc, x_words, x_scales, w1, w2, arr, unit, 
                 )
             nc.scalar.copy(result[:], obank[:, 0:n])
             nc.sync.dma_start(out[:, r0 : r0 + n], result[:])
+
+        for t in range(PACK):
+            nc.vector.tensor_scalar(arr_sb[:, t, :], arr_sb[:, t, :], size[:, t : t + 1], None, ALU.mult)
+        fetch_rows(0)
+        fetch_rows(1)
+        for c, n in enumerate(CHUNKS):
+            r0 = starts[c]
+            cols = slice(r0 // 16, (r0 + n) // 16)
+            by_bank = ring.tile([P, PACK, n], F32, name="by_bank", align_bytes=64)
+            ready = ring.tile([P, PACK, n], F32, name="ready", align_bytes=64)
+            hid_grouped[c] = ring.tile([P, n, PACK], BF16, name="hid_grouped", align_bytes=64)
+            for t in range(PACK):
+                look_up((c, t) in ((0, 0), (0, 1),), by_bank[:, t, :], m_sb[t][:], bk_sb[:, cols])
+            steps = [slice(0, 2), slice(2, 4)] if c in (0, 1, 2,) else [slice(t, t + 1) for t in range(PACK)]
+            for i, ts in enumerate(steps):
+                nc.vector.tensor_tensor(ready[:, ts, :], by_row[c][:, ts, :], by_bank[:, ts, :], ALU.max)
+                if i == 0 and c > 0:
+                    finish(c - 1)
+            if c + 2 < len(CHUNKS):
+                fetch_rows(c + 2)
+            nc.vector.tensor_tensor(
+                hid_grouped[c][:].rearrange("p (c i) t -> p c t i", i=2),
+                ready[:].rearrange("p t (c i) -> p c t i", i=2),
+                arr_sb[:, :, r0 : r0 + n].rearrange("p t (c i) -> p c t i", i=2),
+                ALU.subtract,
+            )
+        finish(len(CHUNKS) - 1)

@@ -40,7 +40,7 @@ def tile_picked_ydelayq_wait_p_kernel(tc, x_words, x_scales, w1, w2, arr, unit, 
         w1_raw = [keep.tile([P, PACK, H], F32, name=f"w1_raw{g}", align_bytes=64) for g in range(PASSES)]
         w2_raw = [keep.tile([P, PACK, H], F32, name=f"w2_raw{g}", align_bytes=64) for g in range(PASSES)]
         w3_raw = keep.tile([P, PACK, N], F32, name="w3_raw", align_bytes=64)
-        arr_sb = keep.tile([P, PACK, U], F32, name="arr_sb", align_bytes=64)
+        arr_raw = [keep.tile([P, U], F32, name=f"arr_raw{t}", align_bytes=64) for t in range(PACK)]
 
         def load_x(g):
             nc.sync.dma_start(xw_all[g][:].bitcast(I32), x_words[g].rearrange("p n t -> p (n t)").bitcast(I32))
@@ -69,7 +69,7 @@ def tile_picked_ydelayq_wait_p_kernel(tc, x_words, x_scales, w1, w2, arr, unit, 
         for e in range(2):
             nc.sync.dma_start(w3_raw[e:P:2], w3.rearrange("(a t e) n -> e a t n", t=PACK, e=2)[e])
         for t in range(PACK):
-            nc.sync.dma_start(arr_sb[:, t, :], arr.rearrange("(a t e) r -> t a e r", t=PACK, e=2)[t])
+            nc.sync.dma_start(arr_raw[t][:], arr.rearrange("(a t e) r -> t a e r", t=PACK, e=2)[t])
 
         unit_t = unit_sb[:, 0 : 2 * PACK - 1 : 2]
         size = keep.tile([P, PACK], F32, name="size")
@@ -131,11 +131,17 @@ def tile_picked_ydelayq_wait_p_kernel(tc, x_words, x_scales, w1, w2, arr, unit, 
             grouped = keep.tile([P, PACK, P, PACK], BF16, name=f"{name}_bf", align_bytes=64)
             codes = keep.tile([P, H], U32, name=f"{name}_codes", align_bytes=64)
             scales = keep.tile([P, H], U8, name=f"{name}_scales", align_bytes=64)
-            nc.vector.tensor_copy(
-                grouped[:].rearrange("p t (a e) j -> p a t j e", e=2),
-                raw[g][:].rearrange("p j (a t e) -> p a t j e", t=PACK, e=2),
-            )
-            nc.vector.quantize_mx(codes[:].bitcast(FP8X4), scales[:], grouped[:].rearrange("p t m j -> p (t m j)"))
+            for t0 in (0, 2):
+                nc.vector.tensor_copy(
+                    grouped[:].rearrange("p t (a e) j -> p a t j e", e=2)[:, :, t0 : t0 + 2],
+                    raw[g][:].rearrange("p j (a t e) -> p a t j e", t=PACK, e=2)[:, :, t0 : t0 + 2],
+                )
+            for t0 in (0, 2):
+                nc.vector.quantize_mx(
+                    codes[:, t0 * P : (t0 + 2) * P].bitcast(FP8X4),
+                    scales[:, t0 * P : (t0 + 2) * P],
+                    grouped[:, t0 : t0 + 2].rearrange("p t m j -> p (t m j)"),
+                )
             for t in range(PACK):
                 product(banks[t], (grouped, codes, scales), g, t)
 
@@ -168,7 +174,6 @@ def tile_picked_ydelayq_wait_p_kernel(tc, x_words, x_scales, w1, w2, arr, unit, 
             sign[:].rearrange("p (c j i) -> p c j i", c=1, i=1).to_broadcast([P, N // 2, PACK, 2]),
             ALU.mult,
         )
-        nc.vector.quantize_mx(w3_codes[:].bitcast(FP8X4), w3_scales[:], w3_bf[:].rearrange("p n j -> p (n j)"))
 
         starts = [sum(CHUNKS[:c]) for c in range(len(CHUNKS))]
         by_row, hid_grouped = {}, {}
@@ -206,11 +211,15 @@ def tile_picked_ydelayq_wait_p_kernel(tc, x_words, x_scales, w1, w2, arr, unit, 
                     start=True,
                     stop=True,
                 )
-            nc.scalar.copy(result[:], obank[:, 0:n])
+            (nc.vector.tensor_copy if c == len(CHUNKS) - 1 else nc.scalar.copy)(result[:], obank[:, 0:n])
             nc.sync.dma_start(out[:, r0 : r0 + n], result[:])
 
+        arr_sb = keep.tile([P, PACK, U], F32, name="arr_sb", tag="w2q1_bf3", align_bytes=64)
         for t in range(PACK):
-            nc.vector.tensor_scalar(arr_sb[:, t, :], arr_sb[:, t, :], size[:, t : t + 1], None, ALU.mult)
+            if t in (0, 1,):
+                nc.gpsimd.tensor_scalar(arr_sb[:, t, :], arr_raw[t][:], size[:, t : t + 1], 0.0, ALU.mult, ALU.add)
+            else:
+                nc.vector.tensor_scalar(arr_sb[:, t, :], arr_raw[t][:], size[:, t : t + 1], None, ALU.mult)
         fetch_rows(0)
         fetch_rows(1)
         for c, n in enumerate(CHUNKS):
@@ -224,8 +233,12 @@ def tile_picked_ydelayq_wait_p_kernel(tc, x_words, x_scales, w1, w2, arr, unit, 
             steps = [slice(0, 2), slice(2, 4)] if c in (0, 1, 2,) else [slice(t, t + 1) for t in range(PACK)]
             for i, ts in enumerate(steps):
                 nc.vector.tensor_tensor(ready[:, ts, :], by_row[c][:, ts, :], by_bank[:, ts, :], ALU.max)
-                if i == 0 and c > 0:
+                if i == 0 and c == len(CHUNKS) - 1:
                     finish(c - 1)
+            if c == 0:
+                nc.vector.quantize_mx(w3_codes[:].bitcast(FP8X4), w3_scales[:], w3_bf[:].rearrange("p n j -> p (n j)"))
+            elif c < len(CHUNKS) - 1:
+                finish(c - 1)
             if c + 2 < len(CHUNKS):
                 fetch_rows(c + 2)
             nc.vector.tensor_tensor(

from contextlib import ExitStack

import concourse.mybir as mybir

K, T, S, N, H, U = 1024, 1024, 512, 128, 512, 1024
FLOPS = 2 * (2 * K * H * S + H * N * U)

F32 = mybir.dt.float32
BF16 = mybir.dt.bfloat16
I32 = mybir.dt.int32
U32 = mybir.dt.uint32
U16 = mybir.dt.uint16
U8 = mybir.dt.uint8
FP8X4 = mybir.dt.float8_e4m3fn_x4
ALU = mybir.AluOpType
ACT = mybir.ActivationFunctionType

P = 128
PACK = 4
K_PASS = P * PACK
PASSES = K // K_PASS
CHUNKS = (256, 384, 256, 128)
RING = 3
ROW_RING = 2


def tile_picked_ydelayq_wait_p_kernel(tc, x_words, x_scales, w1, w2, arr, unit, w3, offs, bk, rw_, out):
    nc = tc.nc
    with ExitStack() as ctx:
        keep = ctx.enter_context(tc.tile_pool(name="keep", bufs=1))
        ring = ctx.enter_context(tc.tile_pool(name="ring", bufs=RING))
        psum = ctx.enter_context(tc.psum_pool(name="psum", bufs=1))

        offs_sb = keep.tile([P, S // 16], U16, name="offs_sb")
        bk_sb = keep.tile([P, U // 16], U16, name="bk_sb")
        rw_sb = keep.tile([P, U // 16], U16, name="rw_sb")
        xs_all = keep.tile([P, T], U8, name="xs_all", align_bytes=64)
        unit_sb = keep.tile([P, 2 * PACK - 1], F32, name="unit_sb")
        xw_all = [keep.tile([P, T], U32, name=f"xw_all{g}", align_bytes=64) for g in range(PASSES)]
        w1_raw = [keep.tile([P, PACK, H], F32, name=f"w1_raw{g}", align_bytes=64) for g in range(PASSES)]
        w2_raw = [keep.tile([P, PACK, H], F32, name=f"w2_raw{g}", align_bytes=64) for g in range(PASSES)]
        w3_raw = keep.tile([P, PACK, N], F32, name="w3_raw", align_bytes=64)
        arr_raw = [keep.tile([P, U], F32, name=f"arr_raw{t}", align_bytes=64) for t in range(PACK)]

        def load_x(g):
            nc.sync.dma_start(xw_all[g][:].bitcast(I32), x_words[g].rearrange("p n t -> p (n t)").bitcast(I32))

        def load_w(raw, w, g):
            nc.sync.dma_start(raw[g][:], w[g * K_PASS : (g + 1) * K_PASS, :].rearrange("(p j) c -> p j c", j=PACK))

        nc.gpsimd.memset(xs_all[:].bitcast(I32), 0)
        nc.sync.dma_start(offs_sb[:], offs)
        load_x(0)
        for q in range(4):
            nc.sync.dma_start(
                xs_all[32 * q : 32 * q + 4 * PASSES, :].bitcast(I32),
                x_scales[:, 4 * q : 4 * q + 4, :].bitcast(I32),
            )
        load_w(w1_raw, w1, 0)
        load_x(1)
        unit_rows = unit.rearrange("(a s) o -> a (s o)", s=2 * PACK)
        for e in range(2):
            nc.sync.dma_start(unit_sb[e:P:2, :], unit_rows[:, e : e + 2 * PACK - 1])
        load_w(w1_raw, w1, 1)
        nc.sync.dma_start(rw_sb[:], rw_)
        load_w(w2_raw, w2, 0)
        load_w(w2_raw, w2, 1)
        nc.sync.dma_start(bk_sb[:], bk)
        for e in range(2):
            nc.sync.dma_start(w3_raw[e:P:2], w3.rearrange("(a t e) n -> e a t n", t=PACK, e=2)[e])
        for t in range(PACK):
            nc.sync.dma_start(arr_raw[t][:], arr.rearrange("(a t e) r -> t a e r", t=PACK, e=2)[t])

        unit_t = unit_sb[:, 0 : 2 * PACK - 1 : 2]
        size = keep.tile([P, PACK], F32, name="size")
        step = keep.tile([P, PACK], F32, name="step")
        sign = keep.tile([P, PACK], F32, name="sign")
        nc.scalar.activation(size[:], unit_t, ACT.Abs)
        nc.gpsimd.tensor_scalar(step[:], unit_t, 0.0, 2.0, ALU.is_ge, ALU.mult)
        nc.gpsimd.tensor_scalar(sign[:], step[:], 1.0, -1.0, ALU.mult, ALU.add)

        xw = {}
        xs = keep.tile([P, S], U8, name="xs", align_bytes=64)

        def gather_x(g, tag):
            xw[g] = keep.tile([P, S], U32, name=f"xw{g}", tag=tag, align_bytes=64)
            nc.vector.tensor_copy(xw[g][:], xw_all[g][:].indirect(offs_sb[:]))

        def new_weight(name):
            grouped = [keep.tile([P, P, PACK], BF16, name=f"{name}_bf{t}", tag=f"{name}_bf{t}", align_bytes=64) for t in range(PACK)]
            codes = keep.tile([P, H], U32, name=f"{name}_codes", align_bytes=64)
            scales = keep.tile([P, H], U8, name=f"{name}_scales", align_bytes=64)
            return grouped, codes, scales

        def cast(on_vector, weight, raw, t):
            copy = nc.vector.tensor_copy if on_vector else nc.scalar.copy
            copy(
                weight[0][t][:].rearrange("p (a e) j -> p a j e", e=2),
                raw[:].rearrange("p j (a t e) -> p t a j e", t=PACK, e=2)[:, t],
            )

        def quantize(weight, t):
            grouped, codes, scales = weight
            nc.vector.quantize_mx(
                codes[:, t * P : (t + 1) * P].bitcast(FP8X4),
                scales[:, t * P : (t + 1) * P],
                grouped[t][:].rearrange("p m j -> p (m j)"),
            )

        def product(bank, weight, g, t):
            nc.tensor.matmul_mx(
                bank[:],
                lhsT=weight[1][:, t * P : (t + 1) * P].bitcast(FP8X4),
                lhsT_scale=weight[2][:, t * P : (t + 1) * P],
                rhs=xw[g][:].bitcast(FP8X4),
                rhs_scale=xs[4 * g : P, :],
                start=(g == 0),
                stop=(g == PASSES - 1),
            )

        def weight_pass(banks, name, raw, g, on_vector):
            weight = new_weight(name)
            for t in range(PACK + 1):
                if t < PACK:
                    cast(t in on_vector, weight, raw[g], t)
                if t > 0:
                    quantize(weight, t - 1)
                    product(banks[t - 1], weight, g, t - 1)

        def wide_pass(banks, name, raw, g):
            grouped = keep.tile([P, PACK, P, PACK], BF16, name=f"{name}_bf", align_bytes=64)
            codes = keep.tile([P, H], U32, name=f"{name}_codes", align_bytes=64)
            scales = keep.tile([P, H], U8, name=f"{name}_scales", align_bytes=64)
            for t0 in (0, 2):
                nc.vector.tensor_copy(
                    grouped[:].rearrange("p t (a e) j -> p a t j e", e=2)[:, :, t0 : t0 + 2],
                    raw[g][:].rearrange("p j (a t e) -> p a t j e", t=PACK, e=2)[:, :, t0 : t0 + 2],
                )
            for t0 in (0, 2):
                nc.vector.quantize_mx(
                    codes[:, t0 * P : (t0 + 2) * P].bitcast(FP8X4),
                    scales[:, t0 * P : (t0 + 2) * P],
                    grouped[:, t0 : t0 + 2].rearrange("p t m j -> p (t m j)"),
                )
            for t in range(PACK):
                product(banks[t], (grouped, codes, scales), g, t)

        ybank = [psum.tile([P, S], F32, name=f"ybank{t}", tag=f"bank{t}") for t in range(PACK)]
        zbank = [psum.tile([P, S], F32, name=f"zbank{t}", tag=f"bank{PACK + t}") for t in range(PACK)]
        y_sb = [keep.tile([P, S], F32, name=f"y_sb{t}", align_bytes=64) for t in range(PACK)]
        m_sb = [keep.tile([P, S], F32, name=f"m_sb{t}", align_bytes=64) for t in range(PACK)]

        gather_x(0, "xw0")
        nc.vector.tensor_copy(xs[:], xs_all[:].indirect(offs_sb[:]))
        weight_pass(ybank, "w1q0", w1_raw, 0, (1, 3,))
        gather_x(1, "w1q0_bf3")
        weight_pass(ybank, "w1q1", w1_raw, 1, (0, 2,))
        for t in range(PACK):
            if t in (1,):
                nc.vector.tensor_scalar(y_sb[t][:], ybank[t][:], size[:, t : t + 1], None, ALU.mult)
            else:
                nc.scalar.activation(y_sb[t][:], ybank[t][:], ACT.Copy, scale=size[:, t : t + 1])
        wide_pass(zbank, "w2q0", w2_raw, 0)
        weight_pass(zbank, "w2q1", w2_raw, 1, range(PACK))
        for t in range(PACK):
            nc.vector.scalar_tensor_tensor(m_sb[t][:], zbank[t][:], size[:, t : t + 1], y_sb[t][:], ALU.mult, ALU.max)

        w3_bf = keep.tile([P, N, PACK], BF16, name="w3_bf", align_bytes=64)
        w3_codes = keep.tile([P, N], U32, name="w3_codes", align_bytes=64)
        w3_scales = keep.tile([P, N], U8, name="w3_scales", align_bytes=64)
        nc.vector.tensor_tensor(
            w3_bf[:].rearrange("p (c i) j -> p c j i", i=2),
            w3_raw[:].rearrange("p j (c i) -> p c j i", i=2),
            sign[:].rearrange("p (c j i) -> p c j i", c=1, i=1).to_broadcast([P, N // 2, PACK, 2]),
            ALU.mult,
        )

        starts = [sum(CHUNKS[:c]) for c in range(len(CHUNKS))]
        by_row, hid_grouped = {}, {}

        def look_up(on_vector, dst, window, offsets):
            if on_vector:
                nc.vector.tensor_copy(dst, window.indirect(offsets))
            else:
                nc.scalar.activation(dst, window.indirect(offsets), ACT.Copy)

        def fetch_rows(c):
            n = CHUNKS[c]
            cols = slice(starts[c] // 16, (starts[c] + n) // 16)
            by_row[c] = ring.tile([P, PACK, n], F32, name="by_row", align_bytes=64, bufs=ROW_RING)
            for t in range(PACK):
                look_up((c, t) in (), by_row[c][:, t, :], y_sb[t][:], rw_sb[:, cols])

        def finish(c):
            n, r0 = CHUNKS[c], starts[c]
            hid_codes = ring.tile([P, n], U32, name="hid_codes", align_bytes=64)
            hid_scales = ring.tile([P, n], U8, name="hid_scales", align_bytes=64)
            result = ring.tile([P, n], F32, name="result", align_bytes=64)
            nc.vector.quantize_mx(
                hid_codes[:].bitcast(FP8X4), hid_scales[:], hid_grouped[c][:].rearrange("p r t -> p (r t)")
            )
            obank = psum.tile([P, S], F32, name=f"obank{c}", tag=f"bank{c % PACK}")
            for n0 in range(0, n, 256):
                n1 = min(n, n0 + 256)
                nc.tensor.matmul_mx(
                    obank[:, n0:n1],
                    lhsT=w3_codes[:].bitcast(FP8X4),
                    lhsT_scale=w3_scales[:],
                    rhs=hid_codes[:, n0:n1].bitcast(FP8X4),
                    rhs_scale=hid_scales[:, n0:n1],
                    start=True,
                    stop=True,
                )
            (nc.vector.tensor_copy if c == len(CHUNKS) - 1 else nc.scalar.copy)(result[:], obank[:, 0:n])
            nc.sync.dma_start(out[:, r0 : r0 + n], result[:])

        arr_sb = keep.tile([P, PACK, U], F32, name="arr_sb", tag="w2q1_bf3", align_bytes=64)
        for t in range(PACK):
            if t in (0, 1,):
                nc.gpsimd.tensor_scalar(arr_sb[:, t, :], arr_raw[t][:], size[:, t : t + 1], 0.0, ALU.mult, ALU.add)
            else:
                nc.vector.tensor_scalar(arr_sb[:, t, :], arr_raw[t][:], size[:, t : t + 1], None, ALU.mult)
        fetch_rows(0)
        fetch_rows(1)
        for c, n in enumerate(CHUNKS):
            r0 = starts[c]
            cols = slice(r0 // 16, (r0 + n) // 16)
            by_bank = ring.tile([P, PACK, n], F32, name="by_bank", align_bytes=64)
            ready = ring.tile([P, PACK, n], F32, name="ready", align_bytes=64)
            hid_grouped[c] = ring.tile([P, n, PACK], BF16, name="hid_grouped", align_bytes=64)
            for t in range(PACK):
                look_up((c, t) in ((0, 0), (0, 1),), by_bank[:, t, :], m_sb[t][:], bk_sb[:, cols])
            steps = [slice(0, 2), slice(2, 4)] if c in (0, 1, 2,) else [slice(t, t + 1) for t in range(PACK)]
            for i, ts in enumerate(steps):
                nc.vector.tensor_tensor(ready[:, ts, :], by_row[c][:, ts, :], by_bank[:, ts, :], ALU.max)
                if i == 0 and c == len(CHUNKS) - 1:
                    finish(c - 1)
            if c == 0:
                nc.vector.quantize_mx(w3_codes[:].bitcast(FP8X4), w3_scales[:], w3_bf[:].rearrange("p n j -> p (n j)"))
            elif c < len(CHUNKS) - 1:
                finish(c - 1)
            if c + 2 < len(CHUNKS):
                fetch_rows(c + 2)
            nc.vector.tensor_tensor(
                hid_grouped[c][:].rearrange("p (c i) t -> p c t i", i=2),
                ready[:].rearrange("p t (c i) -> p c t i", i=2),
                arr_sb[:, :, r0 : r0 + n].rearrange("p t (c i) -> p c t i", i=2),
                ALU.subtract,
            )
        finish(len(CHUNKS) - 1)
